import numpy as np
import ml_dtypes


def mxq(x, axis, fmt="e4m3"):
    dtype, down = {"e4m3": (ml_dtypes.float8_e4m3fn, 7), "e5m2": (ml_dtypes.float8_e5m2, 14)}[fmt]
    v = np.moveaxis(np.asarray(x, np.float32).astype(ml_dtypes.bfloat16).astype(np.float64), axis, -1)
    blocks = v.reshape(v.shape[:-1] + (-1, 32))
    amax = np.abs(blocks).max(-1, keepdims=True)
    byte = np.maximum(np.where(amax > 0, np.frexp(amax)[1] - 1 + 127, 0) - down, 1)
    scale = np.exp2(byte - 127.0)
    codes = (blocks / scale).astype(np.float32).astype(dtype).astype(np.float64)
    return np.moveaxis((codes * scale).reshape(v.shape), -1, axis)


WIDE = False


def mx_kscale(k):
    if not WIDE:
        return np.ones(k)
    levels = np.array([10, -10, 5, -5, 0])
    if k % 512:
        return np.exp2(np.random.permutation(np.resize(levels, k // 32))).repeat(32)
    a = np.empty((k // 512, 16))
    for p in range(k // 512):
        a[p, :8] = np.random.permutation(np.resize(levels, 8))
        for g in range(8):
            far = levels[np.abs(levels - a[p, g]) >= 10]
            a[p, g + 8] = far[np.random.randint(len(far))]
    return np.exp2(a.ravel()).repeat(32)


def f64(x):
    return np.asarray(x).astype(np.float64)


def striped(idx):
    return np.tile(idx.reshape(-1, 16).T, (8, 1)).astype(np.uint16)


def unstriped(offs):
    return offs[:16].T.reshape(-1).astype(np.int64)


def pack_weight(w):
    k, n = w.shape
    w = f64(np.asarray(w, np.float32).astype(ml_dtypes.bfloat16)).reshape(k // 32, 32, n)
    amax = np.abs(w).max(1)
    byte = np.clip(np.where(amax > 0, np.frexp(amax)[1] - 1 + 127 - 7, 1), 1, 254)
    scaled = (w * np.exp2(127.0 - byte)[:, None, :]).reshape(k, n).astype(np.float32)
    words = np.ascontiguousarray(scaled.reshape(k // 512, 128, 4, n).transpose(0, 1, 3, 2)).astype(ml_dtypes.float8_e4m3fn).view(np.uint8)
    return words, np.ascontiguousarray(byte.astype(np.uint8).reshape(k // 512, 16, n))


def unpack_weight(words, scales):
    g, p, n, _ = words.shape
    vals = np.ascontiguousarray(words).view(ml_dtypes.float8_e4m3fn).astype(np.float64) * np.repeat(np.exp2(scales.astype(np.float64) - 127.0), 8, axis=1)[..., None]
    return vals.transpose(0, 1, 3, 2).reshape(g * 512, n)


K, T, S, N = 512, 4096, 1024, 256


def setup_inputs():
    n = np.random.standard_normal
    s = mx_kscale(K)[:, None]
    packed_xT = pack_weight(n((K, T)) * s)
    return {
        "x_words": packed_xT[0],
        "x_scales": packed_xT[1],
        "w1": (n((K, N)) / np.sqrt(K) / s).astype(np.float32),
        "w2": (n((K, N)) / np.sqrt(K) / s).astype(np.float32),
        "w3": (n((K, N)) / np.sqrt(K) / s).astype(np.float32),
        "offs": striped(np.random.permutation(T)[:S]),
    }


def reference(x_words, x_scales, w1, w2, w3, offs):
    xq = unpack_weight(x_words, x_scales)[:, unstriped(offs)]
    return np.minimum(np.minimum(mxq(f64(w1), 0, "e4m3").T @ xq, mxq(f64(w2), 0, "e4m3").T @ xq), mxq(f64(w3), 0, "e4m3").T @ xq)

@@ -1,0 +1,105 @@
+from contextlib import ExitStack
+
+import concourse.mybir as mybir
+
+K, T, S, N = 512, 4096, 1024, 256
+FLOPS = 3 * 2 * K * N * S
+
+F32 = mybir.dt.float32
+BF16 = mybir.dt.bfloat16
+I32 = mybir.dt.int32
+U32 = mybir.dt.uint32
+U16 = mybir.dt.uint16
+U8 = mybir.dt.uint8
+FP8X4 = mybir.dt.float8_e4m3fn_x4
+MIN = mybir.AluOpType.min
+
+P = 128
+PACK = 4
+M_TILE = 128
+S_TILE = 512
+
+
+def tile_picked_maxout_min_p_kernel(tc, x_words, x_scales, w1, w2, w3, offs, out):
+    nc = tc.nc
+    weights = (w1, w2, w3)
+    m_tiles = N // M_TILE
+    s_tiles = S // S_TILE
+    with ExitStack() as ctx:
+        keep = ctx.enter_context(tc.tile_pool(name="keep", bufs=1))
+        psum = ctx.enter_context(tc.psum_pool(name="psum", bufs=1))
+
+        offsets = keep.tile([P, S // 16], U16, name="offsets")
+        nc.sync.dma_start(offsets[:], offs)
+
+        scale_table = keep.tile([P, T], U8, name="scale_table", align_bytes=64)
+        nc.vector.memset(scale_table[:].bitcast(I32), 0)
+        for q in range(4):
+            nc.scalar.dma_start(scale_table[32 * q : 32 * q + 4, :].bitcast(I32), x_scales[0, 4 * q : 4 * q + 4, :].bitcast(I32))
+
+        word_table = keep.tile([P, T], U32, name="word_table", align_bytes=64)
+        nc.sync.dma_start(word_table[:].bitcast(I32), x_words[0].rearrange("p n t -> p (n t)").bitcast(I32))
+
+        raw = {}
+        for m in range(m_tiles):
+            for i in range(3):
+                raw[i, m] = keep.tile([P, PACK, M_TILE], F32, name=f"raw{i}_{m}", align_bytes=64)
+                nc.sync.dma_start(raw[i, m][:], weights[i][:, m * M_TILE : (m + 1) * M_TILE].rearrange("(p j) n -> p j n", j=PACK))
+
+        x_sc = keep.tile([P, S], U8, name="x_sc", align_bytes=64)
+        nc.vector.tensor_copy(x_sc[:], scale_table[:].indirect(offsets[:]))
+
+        x_codes = {}
+
+        def gather_words(s):
+            x_codes[s] = keep.tile([P, S_TILE], U32, name=f"x_codes{s}", align_bytes=64)
+            cols = S_TILE // 16
+            nc.vector.tensor_copy(x_codes[s][:], word_table[:].indirect(offsets[:, s * cols : (s + 1) * cols]))
+
+        grouped, w_codes, w_sc = {}, {}, {}
+
+        def cast(i, m):
+            grouped[i, m] = keep.tile([P, M_TILE, PACK], BF16, name=f"grouped{i}_{m}", align_bytes=64)
+            nc.scalar.copy(grouped[i, m][:], raw[i, m][:].rearrange("p j n -> p n j"))
+
+        def quantize(i, m):
+            w_codes[i, m] = keep.tile([P, M_TILE], U32, name=f"w_codes{i}_{m}", align_bytes=64)
+            w_sc[i, m] = keep.tile([P, M_TILE], U8, name=f"w_sc{i}_{m}", align_bytes=64)
+            nc.vector.quantize_mx(out=w_codes[i, m][:].bitcast(FP8X4), scales=w_sc[i, m][:], in_=grouped[i, m][:].rearrange("p n j -> p (n j)"))
+
+        def product(i, m, s):
+            acc = psum.tile([M_TILE, S_TILE], F32, name=f"acc{i}", bufs=(3, 3, 2)[i])
+            nc.tensor.matmul_mx(
+                out=acc[:],
+                lhsT=w_codes[i, m][:].bitcast(FP8X4),
+                lhsT_scale=w_sc[i, m][:],
+                rhs=x_codes[s][:].bitcast(FP8X4),
+                rhs_scale=x_sc[:, s * S_TILE : (s + 1) * S_TILE],
+                start=True,
+                stop=True,
+            )
+            return acc
+
+        def out_tile(m, s):
+            first = keep.tile([M_TILE, S_TILE], F32, name=f"first{m}_{s}")
+            nc.scalar.copy(first[:], product(0, m, s)[:])
+            two = keep.tile([M_TILE, S_TILE], F32, name=f"two{m}_{s}")
+            nc.vector.tensor_tensor(two[:], product(1, m, s)[:], first[:], MIN)
+            three = keep.tile([M_TILE, S_TILE], F32, name=f"three{m}_{s}")
+            nc.vector.tensor_tensor(three[:], product(2, m, s)[:], two[:], MIN)
+            nc.sync.dma_start(out[m * M_TILE : (m + 1) * M_TILE, s * S_TILE : (s + 1) * S_TILE], three[:])
+
+        gather_words(0)
+        for i in range(3):
+            cast(i, 0)
+        quantize(0, 0)
+        gather_words(1)
+        quantize(1, 0)
+        quantize(2, 0)
+        out_tile(0, 0)
+        out_tile(0, 1)
+        for i in range(3):
+            cast(i, 1)
+            quantize(i, 1)
+        out_tile(1, 0)
+        out_tile(1, 1)

@@ -32,22 +32,31 @@ def tile_picked_maxout_min_p_kernel(tc, x_words, x_scales, w1, w2, w3, offs, out
         offsets = keep.tile([P, S // 16], U16, name="offsets")
         nc.sync.dma_start(offsets[:], offs)
 
-        scale_table = keep.tile([P, T], U8, name="scale_table", align_bytes=64)
-        nc.vector.memset(scale_table[:].bitcast(I32), 0)
-        for q in range(4):
-            nc.scalar.dma_start(scale_table[32 * q : 32 * q + 4, :].bitcast(I32), x_scales[0, 4 * q : 4 * q + 4, :].bitcast(I32))
+        raw = {}
 
+        def load_weight(i, m, dst=None):
+            raw[i, m] = keep.tile([P, PACK, M_TILE], F32, name=f"raw{i}_{m}", tag="stage", bufs=2, align_bytes=64)[:] if dst is None else dst
+            nc.sync.dma_start(raw[i, m], weights[i][:, m * M_TILE : (m + 1) * M_TILE].rearrange("(p j) n -> p j n", j=PACK))
+
+        scale_table = keep.tile([P, T], U8, name="scale_table", tag="shared", align_bytes=64)
+        nc.vector.memset(scale_table[:].bitcast(I32), 0)
+        x_sc = keep.tile([P, S], U8, name="x_sc", align_bytes=64)
+        nc.vector.memset(x_sc[:].bitcast(I32), 0)
+
+        load_weight(0, 0)
+        nc.sync.dma_start(scale_table[0:P:8, :].bitcast(I32), x_scales[0].bitcast(I32))
+        load_weight(1, 0)
         word_table = keep.tile([P, T], U32, name="word_table", align_bytes=64)
         nc.sync.dma_start(word_table[:].bitcast(I32), x_words[0].rearrange("p n t -> p (n t)").bitcast(I32))
 
-        raw = {}
-        for m in range(m_tiles):
-            for i in range(3):
-                raw[i, m] = keep.tile([P, PACK, M_TILE], F32, name=f"raw{i}_{m}", align_bytes=64)
-                nc.sync.dma_start(raw[i, m][:], weights[i][:, m * M_TILE : (m + 1) * M_TILE].rearrange("(p j) n -> p j n", j=PACK))
+        picked_sc = keep.tile([P, S], U8, name="picked_sc", align_bytes=64)
+        nc.vector.tensor_copy(picked_sc[:], scale_table[:].indirect(offsets[:]))
+        for q in range(4):
+            nc.sync.dma_start(x_sc[32 * q : 32 * q + 4, :].bitcast(I32), picked_sc[32 * q : 32 * q + 32 : 8, :].bitcast(I32))
 
-        x_sc = keep.tile([P, S], U8, name="x_sc", align_bytes=64)
-        nc.vector.tensor_copy(x_sc[:], scale_table[:].indirect(offsets[:]))
+        late = keep.tile([P, 2, PACK, M_TILE], F32, name="late", tag="shared", align_bytes=64)
+        for i in range(1, 3):
+            load_weight(i, 1, late[:, i - 1])
 
         x_codes = {}
 
@@ -60,7 +69,7 @@ def tile_picked_maxout_min_p_kernel(tc, x_words, x_scales, w1, w2, w3, offs, out
 
         def cast(i, m):
             grouped[i, m] = keep.tile([P, M_TILE, PACK], BF16, name=f"grouped{i}_{m}", align_bytes=64)
-            nc.scalar.copy(grouped[i, m][:], raw[i, m][:].rearrange("p j n -> p n j"))
+            nc.scalar.copy(grouped[i, m][:], raw[i, m].rearrange("p j n -> p n j"))
 
         def quantize(i, m):
             w_codes[i, m] = keep.tile([P, M_TILE], U32, name=f"w_codes{i}_{m}", align_bytes=64)
@@ -80,26 +89,45 @@ def tile_picked_maxout_min_p_kernel(tc, x_words, x_scales, w1, w2, w3, offs, out
             )
             return acc
 
-        def out_tile(m, s):
-            first = keep.tile([M_TILE, S_TILE], F32, name=f"first{m}_{s}")
-            nc.scalar.copy(first[:], product(0, m, s)[:])
-            two = keep.tile([M_TILE, S_TILE], F32, name=f"two{m}_{s}")
-            nc.vector.tensor_tensor(two[:], product(1, m, s)[:], first[:], MIN)
+        first, two = {}, {}
+
+        def copy_first(m, s):
+            first[m, s] = keep.tile([M_TILE, S_TILE], F32, name=f"first{m}_{s}", tag="stage", bufs=2, align_bytes=64) if m == 0 else keep.tile([M_TILE, S_TILE], F32, name=f"first{m}_{s}")
+            nc.scalar.copy(first[m, s][:], product(0, m, s)[:])
+
+        def min_second(m, s):
+            two[m, s] = keep.tile([M_TILE, S_TILE], F32, name=f"two{m}_{s}")
+            nc.vector.tensor_tensor(two[m, s][:], product(1, m, s)[:], first[m, s][:], MIN)
+
+        def min_third(m, s):
             three = keep.tile([M_TILE, S_TILE], F32, name=f"three{m}_{s}")
-            nc.vector.tensor_tensor(three[:], product(2, m, s)[:], two[:], MIN)
+            nc.vector.tensor_tensor(three[:], product(2, m, s)[:], two[m, s][:], MIN)
             nc.sync.dma_start(out[m * M_TILE : (m + 1) * M_TILE, s * S_TILE : (s + 1) * S_TILE], three[:])
 
-        gather_words(0)
-        for i in range(3):
+        for i in range(2):
             cast(i, 0)
-        quantize(0, 0)
+            quantize(i, 0)
+        load_weight(2, 0)
+        load_weight(0, 1)
+        gather_words(0)
         gather_words(1)
-        quantize(1, 0)
+        cast(2, 0)
         quantize(2, 0)
-        out_tile(0, 0)
-        out_tile(0, 1)
-        for i in range(3):
-            cast(i, 1)
-            quantize(i, 1)
-        out_tile(1, 0)
-        out_tile(1, 1)
+        copy_first(0, 0)
+        min_second(0, 0)
+        cast(0, 1)
+        copy_first(0, 1)
+        min_second(0, 1)
+        quantize(0, 1)
+        cast(1, 1)
+        min_third(0, 0)
+        quantize(1, 1)
+        copy_first(1, 0)
+        cast(2, 1)
+        min_third(0, 1)
+        min_second(1, 0)
+        quantize(2, 1)
+        copy_first(1, 1)
+        min_second(1, 1)
+        min_third(1, 0)
+        min_third(1, 1)

@@ -18,34 +18,32 @@ P = 128
 PACK = 4
 M_TILE = 128
 S_TILE = 512
+WARM = 8
 
 
 def tile_picked_maxout_min_p_kernel(tc, x_words, x_scales, w1, w2, w3, offs, out):
     nc = tc.nc
     weights = (w1, w2, w3)
-    m_tiles = N // M_TILE
-    s_tiles = S // S_TILE
     with ExitStack() as ctx:
         keep = ctx.enter_context(tc.tile_pool(name="keep", bufs=1))
         psum = ctx.enter_context(tc.psum_pool(name="psum", bufs=1))
 
-        offsets = keep.tile([P, S // 16], U16, name="offsets")
-        nc.sync.dma_start(offsets[:], offs)
-
         raw = {}
 
-        def load_weight(i, m, dst=None):
-            raw[i, m] = keep.tile([P, PACK, M_TILE], F32, name=f"raw{i}_{m}", tag="stage", bufs=2, align_bytes=64)[:] if dst is None else dst
-            nc.sync.dma_start(raw[i, m], weights[i][:, m * M_TILE : (m + 1) * M_TILE].rearrange("(p j) n -> p j n", j=PACK))
+        def load_weight(i, m, tag):
+            raw[i, m] = keep.tile([P, PACK, M_TILE], F32, name=f"raw{i}_{m}", tag=tag, align_bytes=64)
+            nc.sync.dma_start(raw[i, m][:], weights[i][:, m * M_TILE : (m + 1) * M_TILE].rearrange("(p j) n -> p j n", j=PACK))
 
-        scale_table = keep.tile([P, T], U8, name="scale_table", tag="shared", align_bytes=64)
+        scale_table = keep.tile([P, T], U8, name="scale_table", tag="table", align_bytes=64)
         nc.vector.memset(scale_table[:].bitcast(I32), 0)
         x_sc = keep.tile([P, S], U8, name="x_sc", align_bytes=64)
         nc.vector.memset(x_sc[:].bitcast(I32), 0)
 
-        load_weight(0, 0)
+        load_weight(0, 0, "early0")
+        offsets = keep.tile([P, S // 16], U16, name="offsets")
+        nc.sync.dma_start(offsets[:], offs)
         nc.sync.dma_start(scale_table[0:P:8, :].bitcast(I32), x_scales[0].bitcast(I32))
-        load_weight(1, 0)
+        load_weight(1, 0, "early1")
         word_table = keep.tile([P, T], U32, name="word_table", align_bytes=64)
         nc.sync.dma_start(word_table[:].bitcast(I32), x_words[0].rearrange("p n t -> p (n t)").bitcast(I32))
 
@@ -54,9 +52,10 @@ def tile_picked_maxout_min_p_kernel(tc, x_words, x_scales, w1, w2, w3, offs, out
         for q in range(4):
             nc.sync.dma_start(x_sc[32 * q : 32 * q + 4, :].bitcast(I32), picked_sc[32 * q : 32 * q + 32 : 8, :].bitcast(I32))
 
-        late = keep.tile([P, 2, PACK, M_TILE], F32, name="late", tag="shared", align_bytes=64)
-        for i in range(1, 3):
-            load_weight(i, 1, late[:, i - 1])
+        load_weight(2, 0, "late")
+        load_weight(0, 1, "stage00")
+        load_weight(1, 1, "stage01")
+        load_weight(2, 1, "stage10")
 
         x_codes = {}
 
@@ -69,15 +68,18 @@ def tile_picked_maxout_min_p_kernel(tc, x_words, x_scales, w1, w2, w3, offs, out
 
         def cast(i, m):
             grouped[i, m] = keep.tile([P, M_TILE, PACK], BF16, name=f"grouped{i}_{m}", align_bytes=64)
-            nc.scalar.copy(grouped[i, m][:], raw[i, m].rearrange("p j n -> p n j"))
+            nc.scalar.copy(grouped[i, m][:].rearrange("p (c i) j -> p c j i", i=4), raw[i, m][:].rearrange("p j (c i) -> p c j i", i=4))
 
         def quantize(i, m):
-            w_codes[i, m] = keep.tile([P, M_TILE], U32, name=f"w_codes{i}_{m}", align_bytes=64)
+            w_codes[i, m] = keep.tile([P, M_TILE], U32, name=f"w_codes{i}_{m}", tag="table" if (i, m) == (0, 0) else f"w_codes{i}_{m}", align_bytes=64)
             w_sc[i, m] = keep.tile([P, M_TILE], U8, name=f"w_sc{i}_{m}", align_bytes=64)
             nc.vector.quantize_mx(out=w_codes[i, m][:].bitcast(FP8X4), scales=w_sc[i, m][:], in_=grouped[i, m][:].rearrange("p n j -> p (n j)"))
 
+        def bank(i):
+            return psum.tile([M_TILE, S_TILE], F32, name=f"acc{i}", bufs=(3, 3, 2)[i])
+
         def product(i, m, s):
-            acc = psum.tile([M_TILE, S_TILE], F32, name=f"acc{i}", bufs=(3, 3, 2)[i])
+            acc = bank(i)
             nc.tensor.matmul_mx(
                 out=acc[:],
                 lhsT=w_codes[i, m][:].bitcast(FP8X4),
@@ -91,43 +93,59 @@ def tile_picked_maxout_min_p_kernel(tc, x_words, x_scales, w1, w2, w3, offs, out
 
         first, two = {}, {}
 
-        def copy_first(m, s):
-            first[m, s] = keep.tile([M_TILE, S_TILE], F32, name=f"first{m}_{s}", tag="stage", bufs=2, align_bytes=64) if m == 0 else keep.tile([M_TILE, S_TILE], F32, name=f"first{m}_{s}")
-            nc.scalar.copy(first[m, s][:], product(0, m, s)[:])
+        def copy_first(m, s, acc):
+            first[m, s] = keep.tile([M_TILE, S_TILE], F32, name=f"first{m}_{s}", tag=f"stage{m}{s}", align_bytes=64)
+            nc.scalar.copy(first[m, s][:], acc[:])
 
-        def min_second(m, s):
-            two[m, s] = keep.tile([M_TILE, S_TILE], F32, name=f"two{m}_{s}")
-            nc.vector.tensor_tensor(two[m, s][:], product(1, m, s)[:], first[m, s][:], MIN)
+        def min_second(m, s, acc, cols):
+            two[m, s, cols.start] = keep.tile([M_TILE, cols.stop - cols.start], F32, name=f"two{m}_{s}_{cols.start}")
+            nc.vector.tensor_tensor(two[m, s, cols.start][:], acc[:, cols], first[m, s][:, cols], MIN)
 
-        def min_third(m, s):
-            three = keep.tile([M_TILE, S_TILE], F32, name=f"three{m}_{s}")
-            nc.vector.tensor_tensor(three[:], product(2, m, s)[:], two[m, s][:], MIN)
-            nc.sync.dma_start(out[m * M_TILE : (m + 1) * M_TILE, s * S_TILE : (s + 1) * S_TILE], three[:])
+        def min_third(m, s, acc, cols):
+            three = keep.tile([M_TILE, cols.stop - cols.start], F32, name=f"three{m}_{s}_{cols.start}")
+            nc.vector.tensor_tensor(three[:], acc[:, cols], two[m, s, cols.start][:], MIN)
+            nc.sync.dma_start(out[m * M_TILE : (m + 1) * M_TILE, s * S_TILE + cols.start : s * S_TILE + cols.stop], three[:])
+
+        whole = slice(0, S_TILE)
+        left, right = slice(0, S_TILE // 2), slice(S_TILE // 2, S_TILE)
 
         for i in range(2):
             cast(i, 0)
             quantize(i, 0)
-        load_weight(2, 0)
-        load_weight(0, 1)
+        spare = bank(2)
+        for r in range(WARM):
+            nc.tensor.matmul_mx(
+                out=spare[:, (r % 4) * M_TILE : (r % 4 + 1) * M_TILE],
+                lhsT=w_codes[0, 0][:].bitcast(FP8X4),
+                lhsT_scale=w_sc[0, 0][:],
+                rhs=w_codes[1, 0][:].bitcast(FP8X4),
+                rhs_scale=x_sc[:, 0:M_TILE],
+                start=True,
+                stop=True,
+            )
         gather_words(0)
         gather_words(1)
         cast(2, 0)
         quantize(2, 0)
-        copy_first(0, 0)
-        min_second(0, 0)
         cast(0, 1)
-        copy_first(0, 1)
-        min_second(0, 1)
         quantize(0, 1)
+        copy_first(0, 0, product(0, 0, 0))
+        min_second(0, 0, product(1, 0, 0), whole)
         cast(1, 1)
-        min_third(0, 0)
+        copy_first(0, 1, product(0, 0, 1))
         quantize(1, 1)
-        copy_first(1, 0)
+        min_third(0, 0, product(2, 0, 0), whole)
+        min_second(0, 1, product(1, 0, 1), whole)
         cast(2, 1)
-        min_third(0, 1)
-        min_second(1, 0)
+        copy_first(1, 0, product(0, 1, 0))
         quantize(2, 1)
-        copy_first(1, 1)
-        min_second(1, 1)
-        min_third(1, 0)
-        min_third(1, 1)
+        min_third(0, 1, product(2, 0, 1), whole)
+        copy_first(1, 1, product(0, 1, 1))
+        min_second(1, 0, product(1, 1, 0), whole)
+        second = product(1, 1, 1)
+        min_second(1, 1, second, left)
+        min_third(1, 0, product(2, 1, 0), whole)
+        min_second(1, 1, second, right)
+        third = product(2, 1, 1)
+        min_third(1, 1, third, left)
+        min_third(1, 1, third, right)

from contextlib import ExitStack

import concourse.mybir as mybir

K, T, S, N = 512, 4096, 1024, 256
FLOPS = 3 * 2 * K * N * S

F32 = mybir.dt.float32
BF16 = mybir.dt.bfloat16
I32 = mybir.dt.int32
U32 = mybir.dt.uint32
U16 = mybir.dt.uint16
U8 = mybir.dt.uint8
FP8X4 = mybir.dt.float8_e4m3fn_x4
MIN = mybir.AluOpType.min

P = 128
PACK = 4
M_TILE = 128
S_TILE = 512
WARM = 8


def tile_picked_maxout_min_p_kernel(tc, x_words, x_scales, w1, w2, w3, offs, out):
    nc = tc.nc
    weights = (w1, w2, w3)
    with ExitStack() as ctx:
        keep = ctx.enter_context(tc.tile_pool(name="keep", bufs=1))
        psum = ctx.enter_context(tc.psum_pool(name="psum", bufs=1))

        raw = {}

        def load_weight(i, m, tag):
            raw[i, m] = keep.tile([P, PACK, M_TILE], F32, name=f"raw{i}_{m}", tag=tag, align_bytes=64)
            nc.sync.dma_start(raw[i, m][:], weights[i][:, m * M_TILE : (m + 1) * M_TILE].rearrange("(p j) n -> p j n", j=PACK))

        scale_table = keep.tile([P, T], U8, name="scale_table", tag="table", align_bytes=64)
        nc.vector.memset(scale_table[:].bitcast(I32), 0)
        x_sc = keep.tile([P, S], U8, name="x_sc", align_bytes=64)
        nc.vector.memset(x_sc[:].bitcast(I32), 0)

        load_weight(0, 0, "early0")
        offsets = keep.tile([P, S // 16], U16, name="offsets")
        nc.sync.dma_start(offsets[:], offs)
        nc.sync.dma_start(scale_table[0:P:8, :].bitcast(I32), x_scales[0].bitcast(I32))
        load_weight(1, 0, "early1")
        word_table = keep.tile([P, T], U32, name="word_table", align_bytes=64)
        nc.sync.dma_start(word_table[:].bitcast(I32), x_words[0].rearrange("p n t -> p (n t)").bitcast(I32))

        picked_sc = keep.tile([P, S], U8, name="picked_sc", align_bytes=64)
        nc.vector.tensor_copy(picked_sc[:], scale_table[:].indirect(offsets[:]))
        for q in range(4):
            nc.sync.dma_start(x_sc[32 * q : 32 * q + 4, :].bitcast(I32), picked_sc[32 * q : 32 * q + 32 : 8, :].bitcast(I32))

        load_weight(2, 0, "late")
        load_weight(0, 1, "stage00")
        load_weight(1, 1, "stage01")
        load_weight(2, 1, "stage10")

        x_codes = {}

        def gather_words(s):
            x_codes[s] = keep.tile([P, S_TILE], U32, name=f"x_codes{s}", align_bytes=64)
            cols = S_TILE // 16
            nc.vector.tensor_copy(x_codes[s][:], word_table[:].indirect(offsets[:, s * cols : (s + 1) * cols]))

        grouped, w_codes, w_sc = {}, {}, {}

        def cast(i, m):
            grouped[i, m] = keep.tile([P, M_TILE, PACK], BF16, name=f"grouped{i}_{m}", align_bytes=64)
            nc.scalar.copy(grouped[i, m][:].rearrange("p (c i) j -> p c j i", i=4), raw[i, m][:].rearrange("p j (c i) -> p c j i", i=4))

        def quantize(i, m):
            w_codes[i, m] = keep.tile([P, M_TILE], U32, name=f"w_codes{i}_{m}", tag="table" if (i, m) == (0, 0) else f"w_codes{i}_{m}", align_bytes=64)
            w_sc[i, m] = keep.tile([P, M_TILE], U8, name=f"w_sc{i}_{m}", align_bytes=64)
            nc.vector.quantize_mx(out=w_codes[i, m][:].bitcast(FP8X4), scales=w_sc[i, m][:], in_=grouped[i, m][:].rearrange("p n j -> p (n j)"))

        def bank(i):
            return psum.tile([M_TILE, S_TILE], F32, name=f"acc{i}", bufs=(3, 3, 2)[i])

        def product(i, m, s):
            acc = bank(i)
            nc.tensor.matmul_mx(
                out=acc[:],
                lhsT=w_codes[i, m][:].bitcast(FP8X4),
                lhsT_scale=w_sc[i, m][:],
                rhs=x_codes[s][:].bitcast(FP8X4),
                rhs_scale=x_sc[:, s * S_TILE : (s + 1) * S_TILE],
                start=True,
                stop=True,
            )
            return acc

        first, two = {}, {}

        def copy_first(m, s, acc):
            first[m, s] = keep.tile([M_TILE, S_TILE], F32, name=f"first{m}_{s}", tag=f"stage{m}{s}", align_bytes=64)
            nc.scalar.copy(first[m, s][:], acc[:])

        def min_second(m, s, acc, cols):
            two[m, s, cols.start] = keep.tile([M_TILE, cols.stop - cols.start], F32, name=f"two{m}_{s}_{cols.start}")
            nc.vector.tensor_tensor(two[m, s, cols.start][:], acc[:, cols], first[m, s][:, cols], MIN)

        def min_third(m, s, acc, cols):
            three = keep.tile([M_TILE, cols.stop - cols.start], F32, name=f"three{m}_{s}_{cols.start}")
            nc.vector.tensor_tensor(three[:], acc[:, cols], two[m, s, cols.start][:], MIN)
            nc.sync.dma_start(out[m * M_TILE : (m + 1) * M_TILE, s * S_TILE + cols.start : s * S_TILE + cols.stop], three[:])

        whole = slice(0, S_TILE)
        left, right = slice(0, S_TILE // 2), slice(S_TILE // 2, S_TILE)

        for i in range(2):
            cast(i, 0)
            quantize(i, 0)
        spare = bank(2)
        for r in range(WARM):
            nc.tensor.matmul_mx(
                out=spare[:, (r % 4) * M_TILE : (r % 4 + 1) * M_TILE],
                lhsT=w_codes[0, 0][:].bitcast(FP8X4),
                lhsT_scale=w_sc[0, 0][:],
                rhs=w_codes[1, 0][:].bitcast(FP8X4),
                rhs_scale=x_sc[:, 0:M_TILE],
                start=True,
                stop=True,
            )
        gather_words(0)
        gather_words(1)
        cast(2, 0)
        quantize(2, 0)
        cast(0, 1)
        quantize(0, 1)
        copy_first(0, 0, product(0, 0, 0))
        min_second(0, 0, product(1, 0, 0), whole)
        cast(1, 1)
        copy_first(0, 1, product(0, 0, 1))
        quantize(1, 1)
        min_third(0, 0, product(2, 0, 0), whole)
        min_second(0, 1, product(1, 0, 1), whole)
        cast(2, 1)
        copy_first(1, 0, product(0, 1, 0))
        quantize(2, 1)
        min_third(0, 1, product(2, 0, 1), whole)
        copy_first(1, 1, product(0, 1, 1))
        min_second(1, 0, product(1, 1, 0), whole)
        second = product(1, 1, 1)
        min_second(1, 1, second, left)
        min_third(1, 0, product(2, 1, 0), whole)
        min_second(1, 1, second, right)
        third = product(2, 1, 1)
        min_third(1, 1, third, left)
        min_third(1, 1, third, right)
